import numpy as np
import ml_dtypes


def mxq(x, axis, fmt="e4m3"):
    dtype, down = {"e4m3": (ml_dtypes.float8_e4m3fn, 7), "e5m2": (ml_dtypes.float8_e5m2, 14)}[fmt]
    v = np.moveaxis(np.asarray(x, np.float32).astype(ml_dtypes.bfloat16).astype(np.float64), axis, -1)
    blocks = v.reshape(v.shape[:-1] + (-1, 32))
    amax = np.abs(blocks).max(-1, keepdims=True)
    byte = np.maximum(np.where(amax > 0, np.frexp(amax)[1] - 1 + 127, 0) - down, 1)
    scale = np.exp2(byte - 127.0)
    codes = (blocks / scale).astype(np.float32).astype(dtype).astype(np.float64)
    return np.moveaxis((codes * scale).reshape(v.shape), -1, axis)


WIDE = False


def mx_kscale(k):
    if not WIDE:
        return np.ones(k)
    levels = np.array([10, -10, 5, -5, 0])
    if k % 512:
        return np.exp2(np.random.permutation(np.resize(levels, k // 32))).repeat(32)
    a = np.empty((k // 512, 16))
    for p in range(k // 512):
        a[p, :8] = np.random.permutation(np.resize(levels, 8))
        for g in range(8):
            far = levels[np.abs(levels - a[p, g]) >= 10]
            a[p, g + 8] = far[np.random.randint(len(far))]
    return np.exp2(a.ravel()).repeat(32)


BF16 = ml_dtypes.bfloat16


def bf(x):
    return np.asarray(x, np.float32).astype(BF16)


def f64(x):
    return np.asarray(x).astype(np.float64)

E4M3FN = np.array([(-1.0 if i & 128 else 1.0) * ((1.0 + (i & 7) / 8.0) * 2.0 ** (((i >> 3) & 15) - 7) if i & 120 else (i & 7) * 2.0 ** -9) for i in range(256)])


def e4m3fn_bytes(y):
    return np.clip(np.asarray(y, np.float64), -448.0, 448.0).astype(np.float32).astype(ml_dtypes.float8_e4m3fn).view(np.uint8)


def e4m3fn_values(b):
    return E4M3FN[b]


M, K, L, T, B = 2048, 1024, 512, 1024, 128


def setup_inputs():
    s, t = mx_kscale(K), mx_kscale(L)
    shapes = np.random.standard_normal((M, K)) * s
    loads = np.random.standard_normal((L, T)) / t[:, None]
    shapes_scale = (np.abs(shapes).reshape(M, K // B, B).max(axis=2) / 448).astype(np.float32)
    loads_scale = (np.abs(loads).reshape(L // B, B, T // B, B).max(axis=(1, 3)) / 448).astype(np.float32)
    shapes_wide = np.repeat(f64(shapes_scale), B, axis=1)
    loads_wide = np.repeat(np.repeat(f64(loads_scale), B, axis=0), B, axis=1)
    return {"shapes_bytes": e4m3fn_bytes(shapes / shapes_wide),
            "shapes_scale": shapes_scale,
            "coords": bf(np.random.standard_normal((T, K)) / np.sqrt(K) / s),
            "flex": bf(np.random.standard_normal((M, L)) / np.sqrt(L) * t),
            "loads_bytes": e4m3fn_bytes(loads / loads_wide),
            "loads_scale": loads_scale,
            "gap": bf(np.random.uniform(0.3, 0.7, (M, 1))),
            "stiffness": bf(np.random.uniform(0.5, 1.5, (M, 1)))}


def reference(shapes_bytes, shapes_scale, coords, flex, loads_bytes, loads_scale, gap, stiffness):
    shapes = e4m3fn_values(shapes_bytes) * np.repeat(f64(shapes_scale), B, axis=1)
    loads = e4m3fn_values(loads_bytes) * np.repeat(np.repeat(f64(loads_scale), B, axis=0), B, axis=1)
    dynamic = mxq(shapes, 1, "e4m3") @ mxq(f64(coords), 1, "e4m3").T
    static = mxq(f64(flex), 1, "e4m3") @ mxq(loads, 0, "e4m3")
    u = dynamic + static
    reaction = f64(stiffness) * np.maximum(u - f64(gap), 0.0)
    return u, reaction

@@ -1,0 +1,524 @@
+from contextlib import ExitStack
+
+import concourse.mybir as mybir
+from concourse.masks import make_identity
+
+M, K, L, T, B = 2048, 1024, 512, 1024, 128
+FLOPS = 2 * M * T * (K + L)
+
+F32 = mybir.dt.float32
+BF16 = mybir.dt.bfloat16
+U32 = mybir.dt.uint32
+U8 = mybir.dt.uint8
+FP8 = mybir.dt.float8_e4m3fn
+FP8X4 = mybir.dt.float8_e4m3fn_x4
+ALU = mybir.AluOpType
+ACT = mybir.ActivationFunctionType
+
+P = 128
+TILES = M // P
+PAIRS = TILES // 2
+HALF = 512
+
+ROW_CHUNKS = ((0, 2), (2, 4), (4, 8), (8, 12), (12, 16))
+
+
+def tile_structural_response_stops_d9_kernel(
+    tc, shapes_bytes, shapes_scale, coords, flex, loads_bytes, loads_scale, gap, stiffness, out_0, out_1
+):
+    nc = tc.nc
+    with ExitStack() as ctx:
+        keep = ctx.enter_context(tc.tile_pool(name="keep", bufs=1))
+        stage = ctx.enter_context(tc.tile_pool(name="stage", bufs=3))
+        outs = ctx.enter_context(tc.tile_pool(name="outs", bufs=4))
+        psum = ctx.enter_context(tc.psum_pool(name="psum", bufs=8))
+        ctx.enter_context(tc.manual_schedule())
+
+        shapes_rows = shapes_bytes.rearrange("(p i) k -> p i k", i=TILES)
+        flex_rows = flex.rearrange("(p i) l -> p i l", i=TILES)
+        u_rows = out_0.rearrange("(p i) t -> p i t", i=TILES)
+        r_rows = out_1.rearrange("(p i) t -> p i t", i=TILES)
+
+        loads_raw = keep.tile([P, 4, T], U8, name="loads_raw", align_bytes=64)
+        ls_all = keep.tile([P, 32], F32, name="ls_all")
+        ls = keep.tile([P, 8], F32, name="ls")
+        ss = keep.tile([P, TILES, 8], F32, name="ss")
+        gap_raw = keep.tile([P, TILES], BF16, name="gap_raw")
+        stiff_raw = keep.tile([P, TILES], BF16, name="stiff_raw")
+        neg_gap = keep.tile([P, TILES], F32, name="neg_gap")
+        stiff_f = keep.tile([P, TILES], F32, name="stiff_f")
+        ident_pool = keep.tile([P, P], F32, name="ident_pool")
+        ident = keep.tile([P, P], F32, name="ident")
+        mov_codes = keep.tile([P, 3, T], U32, name="mov_codes", align_bytes=64)
+        mov_scales = keep.tile([P, 3, T], U8, name="mov_scales", align_bytes=64)
+
+        shapes_raw, flex_raw, coords_raw = {}, {}, {}
+
+        def load_shapes(n):
+            lo, hi = ROW_CHUNKS[n]
+            s_tile = keep.tile([P, hi - lo, K], U8, name="shapes_raw%d" % n, align_bytes=64)
+            nc.sync.dma_start(out=s_tile[:], in_=shapes_rows[:, lo:hi, :])
+            for i in range(lo, hi):
+                shapes_raw[i] = s_tile[:, i - lo, :]
+
+        def load_flex(n):
+            lo, hi = ROW_CHUNKS[n]
+            f_tile = keep.tile([P, hi - lo, L], BF16, name="flex_raw%d" % n, align_bytes=64)
+            nc.sync.dma_start(out=f_tile[:], in_=flex_rows[:, lo:hi, :])
+            for i in range(lo, hi):
+                flex_raw[i] = f_tile[:, i - lo, :]
+
+        def load_coords(c):
+            c_tile = keep.tile([P, 2, K], BF16, name="coords_raw%d" % c, align_bytes=64)
+            nc.sync.dma_start(out=c_tile[:], in_=coords[256 * c : 256 * (c + 1), :].rearrange("(p j) k -> p j k", j=2))
+            coords_raw[c] = c_tile
+
+        nc.scalar.dma_start(out=ls_all[:], in_=loads_scale.rearrange("a b -> (a b)").partition_broadcast(P))
+        nc.scalar.dma_start(out=ss[:], in_=shapes_scale.rearrange("(p i) b -> p i b", i=TILES))
+        idle = keep.tile([P, HALF], BF16, name="idle")
+        idle_bank = psum.tile([P, HALF], F32, name="bank")
+        nc.vector.memset(idle[:], 0.0)
+        make_identity(nc, ident_pool[:])
+        nc.scalar.activation(out=ident[:], in_=ident_pool[:], func=ACT.Copy)
+        for q in range(4):
+            rows = slice(32 * q, 32 * (q + 1))
+            nc.vector.tensor_copy(out=ls[rows, :], in_=ls_all[rows, 8 * q : 8 * (q + 1)])
+
+        loads_wide, loads_grouped, coords_grouped = {}, {}, {}
+        sums = {}
+        wide, turned, grouped, codes, scales, u_out, r_out = {}, {}, {}, {}, {}, {}, {}
+
+        def widen_loads(h, blocks, on_scalar):
+            if h not in loads_wide:
+                loads_wide[h] = keep.tile([P, 4, HALF], BF16, name="loads_wide%d" % h, align_bytes=64)
+            for b in blocks:
+                for t in range(4):
+                    j = 4 * h + b
+                    src = loads_raw[:, t, B * j : B * (j + 1)].bitcast(FP8)
+                    dst = loads_wide[h][:, t, B * b : B * (b + 1)]
+                    if on_scalar:
+                        nc.scalar.activation(out=dst, in_=src, func=ACT.Copy, scale=ls[:, j : j + 1])
+                    else:
+                        nc.vector.tensor_scalar(out=dst, in0=src, scalar1=ls[:, j : j + 1], scalar2=None, op0=ALU.mult)
+
+        def interleave_loads(h):
+            loads_grouped[h] = keep.tile([P, HALF, 4], BF16, name="loads_grouped%d" % h, align_bytes=64)
+            nc.vector.tensor_copy(
+                out=loads_grouped[h][:].rearrange("p (c i) t -> p c t i", i=4),
+                in_=loads_wide[h][:].rearrange("p t (c i) -> p c t i", i=4),
+            )
+
+        def quantize_moving(g, h, src):
+            cols = slice(HALF * h, HALF * (h + 1))
+            nc.vector.quantize_mx(out=mov_codes[:, g, cols].bitcast(FP8X4), scales=mov_scales[:, g, cols], in_=src)
+
+        def quantize_loads(h):
+            quantize_moving(2, h, loads_grouped[h][:].rearrange("p c t -> p (c t)"))
+
+        def turn_coords(c):
+            for g in range(2):
+                bank = psum.tile([P, 2, 2, P], F32, name="bank")
+                for j in range(2):
+                    words = coords_raw[c][:, j, :].bitcast(F32)
+                    for u in range(2):
+                        nc.tensor.transpose(bank[:, j, u, :], words[:, 256 * g + u : 256 * (g + 1) : 2], ident[:])
+                turned["coords", c, g] = bank
+
+        def empty_coords(c):
+            h = c // 2
+            for g in range(2):
+                if (h, g) not in coords_grouped:
+                    coords_grouped[h, g] = keep.tile([P, 2, 1024], BF16, name="coords_grouped%d%d" % (h, g), align_bytes=64)
+                dst = coords_grouped[h, g][:, c % 2, :].bitcast(F32).rearrange("q (p j u) -> q p j u", j=2, u=2)
+                nc.scalar.copy(out=dst, in_=turned["coords", c, g][:].rearrange("q j u p -> q p j u"))
+
+        def quantize_coords(h, g):
+            quantize_moving(g, h, coords_grouped[h, g][:].rearrange("q c n -> q (c n)"))
+
+        def widen_shapes(i):
+            wide[i] = stage.tile([P, 2, 2, P, 2], BF16, name="wide", bufs=6, align_bytes=64)
+            for b in range(8):
+                g, q = divmod(b, 4)
+                src = shapes_raw[i][:, B * b : B * (b + 1)].bitcast(FP8).rearrange("p (w u e) -> p w u e", u=2, e=2)
+                dst = wide[i][:, g, :, 32 * q : 32 * (q + 1), :].rearrange("p u w e -> p w u e")
+                nc.vector.tensor_scalar(out=dst, in0=src, scalar1=ss[:, i, b : b + 1], scalar2=None, op0=ALU.mult)
+
+        def turn_shapes(i):
+            bank = psum.tile([P, 2, 2, P], F32, name="bank")
+            for g in range(2):
+                for u in range(2):
+                    words = wide[i][:, g, u, :, :].rearrange("p w e -> p (w e)").bitcast(F32)
+                    nc.tensor.transpose(bank[:, g, u, :], words, ident[:])
+            turned[i // 2, i % 2] = bank
+
+        def turn_flex(j):
+            bank = psum.tile([P, 2, 2, P], F32, name="bank")
+            for a in range(2):
+                words = flex_raw[2 * j + a].bitcast(F32)
+                for u in range(2):
+                    nc.tensor.transpose(bank[:, a, u, :], words[:, u:256:2], ident[:])
+            turned[j, 2] = bank
+
+        def turn_pair(j):
+            turn_shapes(2 * j)
+            turn_shapes(2 * j + 1)
+            turn_flex(j)
+
+        def empty(j, n):
+            if j not in grouped:
+                grouped[j] = stage.tile([P, 3, 1024], BF16, name="grouped", align_bytes=64)
+            dst = grouped[j][:, n, :].bitcast(F32).rearrange("q (x r u) -> q x r u", x=2, u=2)
+            nc.scalar.copy(out=dst, in_=turned[j, n][:].rearrange("q x u r -> q x r u"))
+
+        def empty_pair(j):
+            for n in range(3):
+                empty(j, n)
+
+        def warm_up(count):
+            for n in range(count):
+                nc.tensor.matmul(idle_bank[:], lhsT=idle[:, :P], rhs=idle[:], start=True, stop=True)
+
+        def open_codes(j):
+            if j not in codes:
+                codes[j] = stage.tile([P, 6 * P], U32, name="codes", align_bytes=64)
+                scales[j] = stage.tile([P, 6 * P], U8, name="scales", align_bytes=64)
+
+        def quantize_shapes(j):
+            open_codes(j)
+            nc.vector.quantize_mx(
+                out=codes[j][:, : 4 * P].bitcast(FP8X4),
+                scales=scales[j][:, : 4 * P],
+                in_=grouped[j][:, 0:2, :].rearrange("q n c -> q (n c)"),
+            )
+
+        def quantize_flex(j):
+            open_codes(j)
+            nc.vector.quantize_mx(
+                out=codes[j][:, 4 * P :].bitcast(FP8X4), scales=scales[j][:, 4 * P :], in_=grouped[j][:, 2, :]
+            )
+
+        def multiply(j, a, h):
+            if j not in u_out:
+                u_out[j] = outs.tile([P, 2, T], F32, name="u_out")
+                r_out[j] = outs.tile([P, 2, T], F32, name="r_out")
+            cols = slice(HALF * h, HALF * (h + 1))
+            bank = psum.tile([P, HALF], F32, name="bank")
+            for g in range(3):
+                slot = 2 * a + g if g < 2 else 4 + a
+                rows = slice(P * slot, P * (slot + 1))
+                nc.tensor.matmul_mx(
+                    out=bank[:],
+                    lhsT=codes[j][:, rows].bitcast(FP8X4),
+                    lhsT_scale=scales[j][:, rows],
+                    rhs=mov_codes[:, g, cols].bitcast(FP8X4),
+                    rhs_scale=mov_scales[:, g, cols],
+                    start=(g == 0),
+                    stop=(g == 2),
+                )
+            sums[j, a, h] = bank
+
+        def drain(j, a, h):
+            cols = slice(HALF * h, HALF * (h + 1))
+            bank = sums[j, a, h]
+            nc.scalar.copy(out=u_out[j][:, a, cols], in_=bank[:])
+
+        def close_gap_scalar(j, a, h):
+            i = 2 * j + a
+            cols = slice(HALF * h, HALF * (h + 1))
+            nc.scalar.activation(
+                out=r_out[j][:, a, cols], in_=sums[j, a, h][:], func=ACT.Relu, bias=neg_gap[:, i : i + 1]
+            )
+
+        def close_gap(j, a, lo, hi):
+            i = 2 * j + a
+            cols = slice(HALF * lo, HALF * hi)
+            nc.vector.tensor_scalar(
+                out=r_out[j][:, a, cols], in0=u_out[j][:, a, cols], scalar1=neg_gap[:, i : i + 1], scalar2=0.0,
+                op0=ALU.add, op1=ALU.max,
+            )
+
+        def react(j, a, lo, hi):
+            i = 2 * j + a
+            cols = slice(HALF * lo, HALF * hi)
+            nc.vector.tensor_scalar(
+                out=r_out[j][:, a, cols], in0=r_out[j][:, a, cols], scalar1=stiff_f[:, i : i + 1], scalar2=None,
+                op0=ALU.mult,
+            )
+
+        def store_u(j, a, lo, hi):
+            cols = slice(HALF * lo, HALF * hi)
+            nc.sync.dma_start(out=u_rows[:, 2 * j + a, cols], in_=u_out[j][:, a, cols])
+
+        def store_r(j, a, lo, hi):
+            cols = slice(HALF * lo, HALF * hi)
+            nc.sync.dma_start(out=r_rows[:, 2 * j + a, cols], in_=r_out[j][:, a, cols])
+
+        def load_loads():
+            nc.sync.dma_start(out=loads_raw[:], in_=loads_bytes.rearrange("(p t) n -> p t n", t=4))
+
+        def load_stops():
+            nc.sync.dma_start(out=gap_raw[:], in_=gap.rearrange("(p i) o -> p (i o)", i=TILES))
+            nc.sync.dma_start(out=stiff_raw[:], in_=stiffness.rearrange("(p i) o -> p (i o)", i=TILES))
+
+        def widen_stops():
+            nc.vector.tensor_scalar(out=neg_gap[:], in0=gap_raw[:], scalar1=-1.0, scalar2=None, op0=ALU.mult)
+            nc.vector.tensor_copy(out=stiff_f[:], in_=stiff_raw[:])
+
+        load_loads()
+        load_shapes(0)
+        load_coords(0)
+        load_flex(0)
+        load_coords(1)
+        load_coords(2)
+        load_coords(3)
+        load_shapes(1)
+        load_flex(1)
+        load_stops()
+        load_shapes(2)
+        load_flex(2)
+        load_shapes(3)
+        load_flex(3)
+        load_shapes(4)
+        load_flex(4)
+        warm_up(11)
+        widen_loads(0, range(4), True)
+        widen_loads(1, [0, 1], True)
+        widen_loads(1, [3], False)
+        widen_shapes(0)
+        widen_loads(1, [2], False)
+        widen_shapes(1)
+        turn_shapes(0)
+        turn_coords(0)
+        turn_shapes(1)
+        warm_up(2)
+        turn_coords(1)
+        turn_flex(0)
+        warm_up(2)
+        interleave_loads(0)
+        interleave_loads(1)
+        empty(0, 0)
+        empty(0, 1)
+        empty_coords(0)
+        empty_coords(1)
+        empty(0, 2)
+        turn_coords(2)
+        turn_coords(3)
+        empty_coords(2)
+        empty_coords(3)
+        quantize_loads(0)
+        quantize_shapes(0)
+        quantize_loads(1)
+        quantize_coords(0, 0)
+        quantize_coords(0, 1)
+        quantize_flex(0)
+        widen_shapes(2)
+        widen_shapes(3)
+        multiply(0, 0, 0)
+        multiply(0, 1, 0)
+        drain(0, 0, 0)
+        store_u(0, 0, 0, 1)
+        drain(0, 1, 0)
+        store_u(0, 1, 0, 1)
+        turn_shapes(2)
+        turn_shapes(3)
+        turn_flex(1)
+        empty(1, 0)
+        empty(1, 1)
+        empty(1, 2)
+        quantize_coords(1, 0)
+        quantize_coords(1, 1)
+        widen_stops()
+        widen_shapes(4)
+        quantize_shapes(1)
+        widen_shapes(5)
+        quantize_flex(1)
+        multiply(0, 0, 1)
+        multiply(0, 1, 1)
+        drain(0, 0, 1)
+        store_u(0, 0, 1, 2)
+        drain(0, 1, 1)
+        store_u(0, 1, 1, 2)
+        close_gap_scalar(0, 1, 1)
+        close_gap(0, 0, 0, 2)
+        close_gap(0, 1, 0, 1)
+        react(0, 0, 0, 2)
+        store_r(0, 0, 0, 2)
+        turn_shapes(4)
+        turn_shapes(5)
+        turn_flex(2)
+        empty(2, 0)
+        empty(2, 1)
+        empty(2, 2)
+        widen_shapes(6)
+        react(0, 1, 0, 2)
+        store_r(0, 1, 0, 2)
+        multiply(1, 0, 0)
+        drain(1, 0, 0)
+        multiply(1, 0, 1)
+        drain(1, 0, 1)
+        multiply(1, 1, 0)
+        drain(1, 1, 0)
+        multiply(1, 1, 1)
+        drain(1, 1, 1)
+        close_gap_scalar(1, 1, 1)
+        quantize_shapes(2)
+        widen_shapes(7)
+        close_gap(1, 0, 0, 2)
+        quantize_flex(2)
+        react(1, 0, 0, 2)
+        store_u(1, 0, 0, 2)
+        store_u(1, 1, 0, 2)
+        store_r(1, 0, 0, 2)
+        turn_shapes(6)
+        turn_shapes(7)
+        turn_flex(3)
+        empty(3, 0)
+        empty(3, 1)
+        empty(3, 2)
+        close_gap(1, 1, 0, 1)
+        widen_shapes(8)
+        react(1, 1, 0, 2)
+        store_r(1, 1, 0, 2)
+        multiply(2, 0, 0)
+        drain(2, 0, 0)
+        multiply(2, 0, 1)
+        drain(2, 0, 1)
+        multiply(2, 1, 0)
+        drain(2, 1, 0)
+        multiply(2, 1, 1)
+        drain(2, 1, 1)
+        close_gap_scalar(2, 1, 1)
+        quantize_shapes(3)
+        widen_shapes(9)
+        close_gap(2, 0, 0, 2)
+        quantize_flex(3)
+        react(2, 0, 0, 2)
+        store_u(2, 0, 0, 2)
+        store_u(2, 1, 0, 2)
+        store_r(2, 0, 0, 2)
+        turn_shapes(8)
+        turn_shapes(9)
+        turn_flex(4)
+        empty(4, 0)
+        empty(4, 1)
+        empty(4, 2)
+        close_gap(2, 1, 0, 1)
+        widen_shapes(10)
+        react(2, 1, 0, 2)
+        store_r(2, 1, 0, 2)
+        multiply(3, 0, 0)
+        drain(3, 0, 0)
+        multiply(3, 0, 1)
+        drain(3, 0, 1)
+        multiply(3, 1, 0)
+        drain(3, 1, 0)
+        multiply(3, 1, 1)
+        drain(3, 1, 1)
+        close_gap_scalar(3, 1, 1)
+        quantize_shapes(4)
+        widen_shapes(11)
+        close_gap(3, 0, 0, 2)
+        quantize_flex(4)
+        react(3, 0, 0, 2)
+        store_u(3, 0, 0, 2)
+        store_u(3, 1, 0, 2)
+        store_r(3, 0, 0, 2)
+        turn_shapes(10)
+        turn_shapes(11)
+        turn_flex(5)
+        empty(5, 0)
+        empty(5, 1)
+        empty(5, 2)
+        close_gap(3, 1, 0, 1)
+        widen_shapes(12)
+        react(3, 1, 0, 2)
+        store_r(3, 1, 0, 2)
+        multiply(4, 0, 0)
+        drain(4, 0, 0)
+        multiply(4, 0, 1)
+        drain(4, 0, 1)
+        multiply(4, 1, 0)
+        drain(4, 1, 0)
+        multiply(4, 1, 1)
+        drain(4, 1, 1)
+        close_gap_scalar(4, 1, 1)
+        quantize_shapes(5)
+        widen_shapes(13)
+        close_gap(4, 0, 0, 2)
+        quantize_flex(5)
+        react(4, 0, 0, 2)
+        store_u(4, 0, 0, 2)
+        store_u(4, 1, 0, 2)
+        store_r(4, 0, 0, 2)
+        turn_shapes(12)
+        turn_shapes(13)
+        turn_flex(6)
+        empty(6, 0)
+        empty(6, 1)
+        empty(6, 2)
+        close_gap(4, 1, 0, 1)
+        widen_shapes(14)
+        react(4, 1, 0, 2)
+        store_r(4, 1, 0, 2)
+        multiply(5, 0, 0)
+        drain(5, 0, 0)
+        multiply(5, 0, 1)
+        drain(5, 0, 1)
+        multiply(5, 1, 0)
+        drain(5, 1, 0)
+        multiply(5, 1, 1)
+        drain(5, 1, 1)
+        close_gap_scalar(5, 1, 1)
+        quantize_shapes(6)
+        widen_shapes(15)
+        close_gap(5, 0, 0, 2)
+        quantize_flex(6)
+        react(5, 0, 0, 2)
+        store_u(5, 0, 0, 2)
+        store_u(5, 1, 0, 2)
+        store_r(5, 0, 0, 2)
+        turn_shapes(14)
+        turn_shapes(15)
+        turn_flex(7)
+        empty(7, 0)
+        empty(7, 1)
+        empty(7, 2)
+        close_gap(5, 1, 0, 1)
+        react(5, 1, 0, 2)
+        store_r(5, 1, 0, 2)
+        multiply(6, 0, 0)
+        drain(6, 0, 0)
+        multiply(6, 0, 1)
+        drain(6, 0, 1)
+        multiply(6, 1, 0)
+        drain(6, 1, 0)
+        multiply(6, 1, 1)
+        drain(6, 1, 1)
+        close_gap_scalar(6, 1, 1)
+        quantize_shapes(7)
+        close_gap(6, 0, 0, 2)
+        quantize_flex(7)
+        react(6, 0, 0, 2)
+        store_u(6, 0, 0, 2)
+        store_u(6, 1, 0, 2)
+        store_r(6, 0, 0, 2)
+        close_gap(6, 1, 0, 1)
+        react(6, 1, 0, 2)
+        store_r(6, 1, 0, 2)
+        multiply(7, 0, 0)
+        drain(7, 0, 0)
+        multiply(7, 0, 1)
+        drain(7, 0, 1)
+        multiply(7, 1, 0)
+        drain(7, 1, 0)
+        multiply(7, 1, 1)
+        drain(7, 1, 1)
+        close_gap_scalar(7, 1, 1)
+        close_gap(7, 0, 0, 2)
+        react(7, 0, 0, 2)
+        store_u(7, 0, 0, 2)
+        store_u(7, 1, 0, 2)
+        store_r(7, 0, 0, 2)
+        close_gap(7, 1, 0, 1)
+        react(7, 1, 0, 2)
+        store_r(7, 1, 0, 2)

@@ -40,8 +40,10 @@ def tile_structural_response_stops_d9_kernel(
         r_rows = out_1.rearrange("(p i) t -> p i t", i=TILES)
 
         loads_raw = keep.tile([P, 4, T], U8, name="loads_raw", align_bytes=64)
-        ls_all = keep.tile([P, 32], F32, name="ls_all")
-        ls = keep.tile([P, 8], F32, name="ls")
+        ls_rows = keep.tile([P, 32], F32, name="ls_rows", align_bytes=64)
+        ls_cols = keep.tile([P, 32], F32, name="ls_cols", align_bytes=64)
+        ls_spread = keep.tile([P, 32], F32, name="ls_spread", align_bytes=64)
+        ls = keep.tile([P, 32], F32, name="ls", align_bytes=64)
         ss = keep.tile([P, TILES, 8], F32, name="ss")
         gap_raw = keep.tile([P, TILES], BF16, name="gap_raw")
         stiff_raw = keep.tile([P, TILES], BF16, name="stiff_raw")
@@ -73,16 +75,8 @@ def tile_structural_response_stops_d9_kernel(
             nc.sync.dma_start(out=c_tile[:], in_=coords[256 * c : 256 * (c + 1), :].rearrange("(p j) k -> p j k", j=2))
             coords_raw[c] = c_tile
 
-        nc.scalar.dma_start(out=ls_all[:], in_=loads_scale.rearrange("a b -> (a b)").partition_broadcast(P))
-        nc.scalar.dma_start(out=ss[:], in_=shapes_scale.rearrange("(p i) b -> p i b", i=TILES))
         idle = keep.tile([P, HALF], BF16, name="idle")
         idle_bank = psum.tile([P, HALF], F32, name="bank")
-        nc.vector.memset(idle[:], 0.0)
-        make_identity(nc, ident_pool[:])
-        nc.scalar.activation(out=ident[:], in_=ident_pool[:], func=ACT.Copy)
-        for q in range(4):
-            rows = slice(32 * q, 32 * (q + 1))
-            nc.vector.tensor_copy(out=ls[rows, :], in_=ls_all[rows, 8 * q : 8 * (q + 1)])
 
         loads_wide, loads_grouped, coords_grouped = {}, {}, {}
         sums = {}
@@ -191,6 +185,11 @@ def tile_structural_response_stops_d9_kernel(
                 in_=grouped[j][:, 0:2, :].rearrange("q n c -> q (n c)"),
             )
 
+        def quantize_tile(j, a):
+            open_codes(j)
+            cols = slice(2 * P * a, 2 * P * (a + 1))
+            nc.vector.quantize_mx(out=codes[j][:, cols].bitcast(FP8X4), scales=scales[j][:, cols], in_=grouped[j][:, a, :])
+
         def quantize_flex(j):
             open_codes(j)
             nc.vector.quantize_mx(
@@ -253,8 +252,28 @@ def tile_structural_response_stops_d9_kernel(
             cols = slice(HALF * lo, HALF * hi)
             nc.sync.dma_start(out=r_rows[:, 2 * j + a, cols], in_=r_out[j][:, a, cols])
 
+        def store_pair(rows, tiles, j):
+            nc.sync.dma_start(out=rows[:, 2 * j : 2 * j + 2, :], in_=tiles[j][:])
+
         def load_loads():
             nc.sync.dma_start(out=loads_raw[:], in_=loads_bytes.rearrange("(p t) n -> p t n", t=4))
+
+        def load_scales():
+            nc.vector.memset(ls_rows[:], 0.0)
+            nc.scalar.dma_start(out=ls_rows[0:P:32, 0:8], in_=loads_scale)
+            nc.scalar.dma_start(out=ss[:], in_=shapes_scale.rearrange("(p i) b -> p i b", i=TILES))
+
+        def prepare_tensor():
+            nc.vector.memset(idle[:], 0.0)
+            make_identity(nc, ident_pool[:])
+
+        def copy_identity():
+            nc.scalar.activation(out=ident[:], in_=ident_pool[:], func=ACT.Copy)
+
+        def spread_loads_scale():
+            nc.vector.transpose(ls_cols[:], ls_rows[:])
+            nc.vector.tensor_copy(out=ls_spread[:], in_=ls_cols[:, 0:1].to_broadcast([P, 32]))
+            nc.vector.transpose(ls[:], ls_spread[:])
 
         def load_stops():
             nc.sync.dma_start(out=gap_raw[:], in_=gap.rearrange("(p i) o -> p (i o)", i=TILES))
@@ -264,7 +283,11 @@ def tile_structural_response_stops_d9_kernel(
             nc.vector.tensor_scalar(out=neg_gap[:], in0=gap_raw[:], scalar1=-1.0, scalar2=None, op0=ALU.mult)
             nc.vector.tensor_copy(out=stiff_f[:], in_=stiff_raw[:])
 
+        load_scales()
+        prepare_tensor()
         load_loads()
+        copy_identity()
+        spread_loads_scale()
         load_shapes(0)
         load_coords(0)
         load_flex(0)
@@ -281,8 +304,12 @@ def tile_structural_response_stops_d9_kernel(
         load_shapes(4)
         load_flex(4)
         warm_up(11)
-        widen_loads(0, range(4), True)
-        widen_loads(1, [0, 1], True)
+        widen_loads(0, [0], True)
+        widen_loads(0, [1], True)
+        widen_loads(0, [2], True)
+        widen_loads(0, [3], True)
+        widen_loads(1, [0], True)
+        widen_loads(1, [1], True)
         widen_loads(1, [3], False)
         widen_shapes(0)
         widen_loads(1, [2], False)
@@ -468,7 +495,6 @@ def tile_structural_response_stops_d9_kernel(
         drain(5, 1, 0)
         multiply(5, 1, 1)
         drain(5, 1, 1)
-        close_gap_scalar(5, 1, 1)
         quantize_shapes(6)
         widen_shapes(15)
         close_gap(5, 0, 0, 2)
@@ -483,7 +509,7 @@ def tile_structural_response_stops_d9_kernel(
         empty(7, 0)
         empty(7, 1)
         empty(7, 2)
-        close_gap(5, 1, 0, 1)
+        close_gap(5, 1, 0, 2)
         react(5, 1, 0, 2)
         store_r(5, 1, 0, 2)
         multiply(6, 0, 0)
@@ -494,7 +520,6 @@ def tile_structural_response_stops_d9_kernel(
         drain(6, 1, 0)
         multiply(6, 1, 1)
         drain(6, 1, 1)
-        close_gap_scalar(6, 1, 1)
         quantize_shapes(7)
         close_gap(6, 0, 0, 2)
         quantize_flex(7)
@@ -502,7 +527,7 @@ def tile_structural_response_stops_d9_kernel(
         store_u(6, 0, 0, 2)
         store_u(6, 1, 0, 2)
         store_r(6, 0, 0, 2)
-        close_gap(6, 1, 0, 1)
+        close_gap(6, 1, 0, 2)
         react(6, 1, 0, 2)
         store_r(6, 1, 0, 2)
         multiply(7, 0, 0)
@@ -513,12 +538,13 @@ def tile_structural_response_stops_d9_kernel(
         drain(7, 1, 0)
         multiply(7, 1, 1)
         drain(7, 1, 1)
-        close_gap_scalar(7, 1, 1)
         close_gap(7, 0, 0, 2)
         react(7, 0, 0, 2)
         store_u(7, 0, 0, 2)
         store_u(7, 1, 0, 2)
         store_r(7, 0, 0, 2)
         close_gap(7, 1, 0, 1)
-        react(7, 1, 0, 2)
+        close_gap(7, 1, 1, 2)
+        react(7, 1, 0, 1)
+        react(7, 1, 1, 2)
         store_r(7, 1, 0, 2)

@@ -40,10 +40,8 @@ def tile_structural_response_stops_d9_kernel(
         r_rows = out_1.rearrange("(p i) t -> p i t", i=TILES)
 
         loads_raw = keep.tile([P, 4, T], U8, name="loads_raw", align_bytes=64)
-        ls_rows = keep.tile([P, 32], F32, name="ls_rows", align_bytes=64)
-        ls_cols = keep.tile([P, 32], F32, name="ls_cols", align_bytes=64)
-        ls_spread = keep.tile([P, 32], F32, name="ls_spread", align_bytes=64)
-        ls = keep.tile([P, 32], F32, name="ls", align_bytes=64)
+        ls_all = keep.tile([P, 32], F32, name="ls_all")
+        ls = keep.tile([P, 8], F32, name="ls")
         ss = keep.tile([P, TILES, 8], F32, name="ss")
         gap_raw = keep.tile([P, TILES], BF16, name="gap_raw")
         stiff_raw = keep.tile([P, TILES], BF16, name="stiff_raw")
@@ -259,9 +257,8 @@ def tile_structural_response_stops_d9_kernel(
             nc.sync.dma_start(out=loads_raw[:], in_=loads_bytes.rearrange("(p t) n -> p t n", t=4))
 
         def load_scales():
-            nc.vector.memset(ls_rows[:], 0.0)
-            nc.scalar.dma_start(out=ls_rows[0:P:32, 0:8], in_=loads_scale)
             nc.scalar.dma_start(out=ss[:], in_=shapes_scale.rearrange("(p i) b -> p i b", i=TILES))
+            nc.scalar.dma_start(out=ls_all[:], in_=loads_scale.rearrange("a b -> (a b)").partition_broadcast(P))
 
         def prepare_tensor():
             nc.vector.memset(idle[:], 0.0)
@@ -271,9 +268,9 @@ def tile_structural_response_stops_d9_kernel(
             nc.scalar.activation(out=ident[:], in_=ident_pool[:], func=ACT.Copy)
 
         def spread_loads_scale():
-            nc.vector.transpose(ls_cols[:], ls_rows[:])
-            nc.vector.tensor_copy(out=ls_spread[:], in_=ls_cols[:, 0:1].to_broadcast([P, 32]))
-            nc.vector.transpose(ls[:], ls_spread[:])
+            for q in range(4):
+                rows = slice(32 * q, 32 * (q + 1))
+                nc.vector.tensor_copy(out=ls[rows, :], in_=ls_all[rows, 8 * q : 8 * (q + 1)])
 
         def load_stops():
             nc.sync.dma_start(out=gap_raw[:], in_=gap.rearrange("(p i) o -> p (i o)", i=TILES))
@@ -285,17 +282,15 @@ def tile_structural_response_stops_d9_kernel(
 
         load_scales()
         prepare_tensor()
-        load_loads()
-        copy_identity()
-        spread_loads_scale()
         load_shapes(0)
+        load_loads()
         load_coords(0)
-        load_flex(0)
         load_coords(1)
+        load_flex(0)
         load_coords(2)
-        load_coords(3)
         load_shapes(1)
         load_flex(1)
+        load_coords(3)
         load_stops()
         load_shapes(2)
         load_flex(2)
@@ -303,45 +298,42 @@ def tile_structural_response_stops_d9_kernel(
         load_flex(3)
         load_shapes(4)
         load_flex(4)
-        warm_up(11)
-        widen_loads(0, [0], True)
-        widen_loads(0, [1], True)
-        widen_loads(0, [2], True)
-        widen_loads(0, [3], True)
-        widen_loads(1, [0], True)
-        widen_loads(1, [1], True)
-        widen_loads(1, [3], False)
+        copy_identity()
+        warm_up(8)
         widen_shapes(0)
-        widen_loads(1, [2], False)
         widen_shapes(1)
+        spread_loads_scale()
         turn_shapes(0)
-        turn_coords(0)
         turn_shapes(1)
         warm_up(2)
+        turn_coords(0)
         turn_coords(1)
-        turn_flex(0)
         warm_up(2)
-        interleave_loads(0)
-        interleave_loads(1)
+        turn_flex(0)
         empty(0, 0)
+        widen_loads(1, [0], True)
         empty(0, 1)
+        widen_loads(0, range(4), False)
+        quantize_shapes(0)
+        interleave_loads(0)
         empty_coords(0)
         empty_coords(1)
-        empty(0, 2)
         turn_coords(2)
-        turn_coords(3)
-        empty_coords(2)
-        empty_coords(3)
-        quantize_loads(0)
-        quantize_shapes(0)
-        quantize_loads(1)
+        widen_loads(1, [1], True)
+        empty(0, 2)
+        widen_loads(1, [2, 3], True)
         quantize_coords(0, 0)
         quantize_coords(0, 1)
+        quantize_loads(0)
         quantize_flex(0)
-        widen_shapes(2)
-        widen_shapes(3)
         multiply(0, 0, 0)
+        turn_coords(3)
         multiply(0, 1, 0)
+        empty_coords(2)
+        empty_coords(3)
+        widen_shapes(2)
+        interleave_loads(1)
+        widen_shapes(3)
         drain(0, 0, 0)
         store_u(0, 0, 0, 1)
         drain(0, 1, 0)
@@ -354,11 +346,11 @@ def tile_structural_response_stops_d9_kernel(
         empty(1, 2)
         quantize_coords(1, 0)
         quantize_coords(1, 1)
-        widen_stops()
+        quantize_loads(1)
         widen_shapes(4)
-        quantize_shapes(1)
         widen_shapes(5)
-        quantize_flex(1)
+        widen_stops()
+        quantize_shapes(1)
         multiply(0, 0, 1)
         multiply(0, 1, 1)
         drain(0, 0, 1)
@@ -367,8 +359,9 @@ def tile_structural_response_stops_d9_kernel(
         store_u(0, 1, 1, 2)
         close_gap_scalar(0, 1, 1)
         close_gap(0, 0, 0, 2)
-        close_gap(0, 1, 0, 1)
+        quantize_flex(1)
         react(0, 0, 0, 2)
+        close_gap(0, 1, 0, 1)
         store_r(0, 0, 0, 2)
         turn_shapes(4)
         turn_shapes(5)

@@ -47,7 +47,6 @@ def tile_structural_response_stops_d9_kernel(
         stiff_raw = keep.tile([P, TILES], BF16, name="stiff_raw")
         neg_gap = keep.tile([P, TILES], F32, name="neg_gap")
         stiff_f = keep.tile([P, TILES], F32, name="stiff_f")
-        ident_pool = keep.tile([P, P], F32, name="ident_pool")
         ident = keep.tile([P, P], F32, name="ident")
         mov_codes = keep.tile([P, 3, T], U32, name="mov_codes", align_bytes=64)
         mov_scales = keep.tile([P, 3, T], U8, name="mov_scales", align_bytes=64)
@@ -73,8 +72,6 @@ def tile_structural_response_stops_d9_kernel(
             nc.sync.dma_start(out=c_tile[:], in_=coords[256 * c : 256 * (c + 1), :].rearrange("(p j) k -> p j k", j=2))
             coords_raw[c] = c_tile
 
-        idle = keep.tile([P, HALF], BF16, name="idle")
-        idle_bank = psum.tile([P, HALF], F32, name="bank")
 
         loads_wide, loads_grouped, coords_grouped = {}, {}, {}
         sums = {}
@@ -135,6 +132,22 @@ def tile_structural_response_stops_d9_kernel(
                 dst = wide[i][:, g, :, 32 * q : 32 * (q + 1), :].rearrange("p u w e -> p w u e")
                 nc.vector.tensor_scalar(out=dst, in0=src, scalar1=ss[:, i, b : b + 1], scalar2=None, op0=ALU.mult)
 
+        def widen_plain(i):
+            wide[i] = keep.tile([P, K], BF16, name="plain%d" % i, align_bytes=64)
+            for b in range(8):
+                cols = slice(B * b, B * (b + 1))
+                nc.scalar.activation(
+                    out=wide[i][:, cols], in_=shapes_raw[i][:, cols].bitcast(FP8), func=ACT.Copy, scale=ss[:, i, b : b + 1]
+                )
+
+        def turn_plain(i):
+            bank = psum.tile([P, 2, 2, P], F32, name="bank")
+            words = wide[i][:].bitcast(F32)
+            for g in range(2):
+                for u in range(2):
+                    nc.tensor.transpose(bank[:, g, u, :], words[:, 256 * g + u : 256 * (g + 1) : 2], ident[:])
+            turned[i // 2, i % 2] = bank
+
         def turn_shapes(i):
             bank = psum.tile([P, 2, 2, P], F32, name="bank")
             for g in range(2):
@@ -165,10 +178,6 @@ def tile_structural_response_stops_d9_kernel(
         def empty_pair(j):
             for n in range(3):
                 empty(j, n)
-
-        def warm_up(count):
-            for n in range(count):
-                nc.tensor.matmul(idle_bank[:], lhsT=idle[:, :P], rhs=idle[:], start=True, stop=True)
 
         def open_codes(j):
             if j not in codes:
@@ -261,11 +270,7 @@ def tile_structural_response_stops_d9_kernel(
             nc.scalar.dma_start(out=ls_all[:], in_=loads_scale.rearrange("a b -> (a b)").partition_broadcast(P))
 
         def prepare_tensor():
-            nc.vector.memset(idle[:], 0.0)
-            make_identity(nc, ident_pool[:])
-
-        def copy_identity():
-            nc.scalar.activation(out=ident[:], in_=ident_pool[:], func=ACT.Copy)
+            make_identity(nc, ident[:])
 
         def spread_loads_scale():
             for q in range(4):
@@ -298,17 +303,13 @@ def tile_structural_response_stops_d9_kernel(
         load_flex(3)
         load_shapes(4)
         load_flex(4)
-        copy_identity()
-        warm_up(8)
         widen_shapes(0)
-        widen_shapes(1)
+        widen_plain(1)
         spread_loads_scale()
         turn_shapes(0)
-        turn_shapes(1)
-        warm_up(2)
+        turn_plain(1)
         turn_coords(0)
         turn_coords(1)
-        warm_up(2)
         turn_flex(0)
         empty(0, 0)
         widen_loads(1, [0], True)
@@ -369,9 +370,6 @@ def tile_structural_response_stops_d9_kernel(
         empty(2, 0)
         empty(2, 1)
         empty(2, 2)
-        widen_shapes(6)
-        react(0, 1, 0, 2)
-        store_r(0, 1, 0, 2)
         multiply(1, 0, 0)
         drain(1, 0, 0)
         multiply(1, 0, 1)
@@ -381,24 +379,24 @@ def tile_structural_response_stops_d9_kernel(
         multiply(1, 1, 1)
         drain(1, 1, 1)
         close_gap_scalar(1, 1, 1)
-        quantize_shapes(2)
+        widen_shapes(6)
+        react(0, 1, 0, 2)
+        store_r(0, 1, 0, 2)
         widen_shapes(7)
+        quantize_shapes(2)
         close_gap(1, 0, 0, 2)
         quantize_flex(2)
-        react(1, 0, 0, 2)
         store_u(1, 0, 0, 2)
         store_u(1, 1, 0, 2)
+        react(1, 0, 0, 2)
         store_r(1, 0, 0, 2)
+        close_gap(1, 1, 0, 1)
         turn_shapes(6)
         turn_shapes(7)
         turn_flex(3)
         empty(3, 0)
         empty(3, 1)
         empty(3, 2)
-        close_gap(1, 1, 0, 1)
-        widen_shapes(8)
-        react(1, 1, 0, 2)
-        store_r(1, 1, 0, 2)
         multiply(2, 0, 0)
         drain(2, 0, 0)
         multiply(2, 0, 1)
@@ -408,24 +406,24 @@ def tile_structural_response_stops_d9_kernel(
         multiply(2, 1, 1)
         drain(2, 1, 1)
         close_gap_scalar(2, 1, 1)
-        quantize_shapes(3)
+        widen_shapes(8)
+        react(1, 1, 0, 2)
+        store_r(1, 1, 0, 2)
         widen_shapes(9)
+        quantize_shapes(3)
         close_gap(2, 0, 0, 2)
         quantize_flex(3)
-        react(2, 0, 0, 2)
         store_u(2, 0, 0, 2)
         store_u(2, 1, 0, 2)
+        react(2, 0, 0, 2)
         store_r(2, 0, 0, 2)
+        close_gap(2, 1, 0, 1)
         turn_shapes(8)
         turn_shapes(9)
         turn_flex(4)
         empty(4, 0)
         empty(4, 1)
         empty(4, 2)
-        close_gap(2, 1, 0, 1)
-        widen_shapes(10)
-        react(2, 1, 0, 2)
-        store_r(2, 1, 0, 2)
         multiply(3, 0, 0)
         drain(3, 0, 0)
         multiply(3, 0, 1)
@@ -435,24 +433,24 @@ def tile_structural_response_stops_d9_kernel(
         multiply(3, 1, 1)
         drain(3, 1, 1)
         close_gap_scalar(3, 1, 1)
-        quantize_shapes(4)
+        widen_shapes(10)
+        react(2, 1, 0, 2)
+        store_r(2, 1, 0, 2)
         widen_shapes(11)
+        quantize_shapes(4)
         close_gap(3, 0, 0, 2)
         quantize_flex(4)
-        react(3, 0, 0, 2)
         store_u(3, 0, 0, 2)
         store_u(3, 1, 0, 2)
+        react(3, 0, 0, 2)
         store_r(3, 0, 0, 2)
+        close_gap(3, 1, 0, 1)
         turn_shapes(10)
         turn_shapes(11)
         turn_flex(5)
         empty(5, 0)
         empty(5, 1)
         empty(5, 2)
-        close_gap(3, 1, 0, 1)
-        widen_shapes(12)
-        react(3, 1, 0, 2)
-        store_r(3, 1, 0, 2)
         multiply(4, 0, 0)
         drain(4, 0, 0)
         multiply(4, 0, 1)
@@ -462,24 +460,24 @@ def tile_structural_response_stops_d9_kernel(
         multiply(4, 1, 1)
         drain(4, 1, 1)
         close_gap_scalar(4, 1, 1)
-        quantize_shapes(5)
+        widen_shapes(12)
+        react(3, 1, 0, 2)
+        store_r(3, 1, 0, 2)
         widen_shapes(13)
+        quantize_shapes(5)
         close_gap(4, 0, 0, 2)
         quantize_flex(5)
-        react(4, 0, 0, 2)
         store_u(4, 0, 0, 2)
         store_u(4, 1, 0, 2)
+        react(4, 0, 0, 2)
         store_r(4, 0, 0, 2)
+        close_gap(4, 1, 0, 1)
         turn_shapes(12)
         turn_shapes(13)
         turn_flex(6)
         empty(6, 0)
         empty(6, 1)
         empty(6, 2)
-        close_gap(4, 1, 0, 1)
-        widen_shapes(14)
-        react(4, 1, 0, 2)
-        store_r(4, 1, 0, 2)
         multiply(5, 0, 0)
         drain(5, 0, 0)
         multiply(5, 0, 1)
@@ -488,23 +486,24 @@ def tile_structural_response_stops_d9_kernel(
         drain(5, 1, 0)
         multiply(5, 1, 1)
         drain(5, 1, 1)
-        quantize_shapes(6)
+        widen_shapes(14)
+        react(4, 1, 0, 2)
+        store_r(4, 1, 0, 2)
         widen_shapes(15)
+        quantize_shapes(6)
         close_gap(5, 0, 0, 2)
         quantize_flex(6)
-        react(5, 0, 0, 2)
         store_u(5, 0, 0, 2)
         store_u(5, 1, 0, 2)
+        react(5, 0, 0, 2)
         store_r(5, 0, 0, 2)
+        close_gap(5, 1, 0, 2)
         turn_shapes(14)
         turn_shapes(15)
         turn_flex(7)
         empty(7, 0)
         empty(7, 1)
         empty(7, 2)
-        close_gap(5, 1, 0, 2)
-        react(5, 1, 0, 2)
-        store_r(5, 1, 0, 2)
         multiply(6, 0, 0)
         drain(6, 0, 0)
         multiply(6, 0, 1)
@@ -513,16 +512,16 @@ def tile_structural_response_stops_d9_kernel(
         drain(6, 1, 0)
         multiply(6, 1, 1)
         drain(6, 1, 1)
+        react(5, 1, 0, 2)
+        store_r(5, 1, 0, 2)
         quantize_shapes(7)
         close_gap(6, 0, 0, 2)
         quantize_flex(7)
-        react(6, 0, 0, 2)
         store_u(6, 0, 0, 2)
         store_u(6, 1, 0, 2)
+        react(6, 0, 0, 2)
         store_r(6, 0, 0, 2)
         close_gap(6, 1, 0, 2)
-        react(6, 1, 0, 2)
-        store_r(6, 1, 0, 2)
         multiply(7, 0, 0)
         drain(7, 0, 0)
         multiply(7, 0, 1)
@@ -531,10 +530,12 @@ def tile_structural_response_stops_d9_kernel(
         drain(7, 1, 0)
         multiply(7, 1, 1)
         drain(7, 1, 1)
+        react(6, 1, 0, 2)
+        store_r(6, 1, 0, 2)
         close_gap(7, 0, 0, 2)
-        react(7, 0, 0, 2)
         store_u(7, 0, 0, 2)
         store_u(7, 1, 0, 2)
+        react(7, 0, 0, 2)
         store_r(7, 0, 0, 2)
         close_gap(7, 1, 0, 1)
         close_gap(7, 1, 1, 2)

from contextlib import ExitStack

import concourse.mybir as mybir
from concourse.masks import make_identity

M, K, L, T, B = 2048, 1024, 512, 1024, 128
FLOPS = 2 * M * T * (K + L)

F32 = mybir.dt.float32
BF16 = mybir.dt.bfloat16
U32 = mybir.dt.uint32
U8 = mybir.dt.uint8
FP8 = mybir.dt.float8_e4m3fn
FP8X4 = mybir.dt.float8_e4m3fn_x4
ALU = mybir.AluOpType
ACT = mybir.ActivationFunctionType

P = 128
TILES = M // P
PAIRS = TILES // 2
HALF = 512

ROW_CHUNKS = ((0, 2), (2, 4), (4, 8), (8, 12), (12, 16))


def tile_structural_response_stops_d9_kernel(
    tc, shapes_bytes, shapes_scale, coords, flex, loads_bytes, loads_scale, gap, stiffness, out_0, out_1
):
    nc = tc.nc
    with ExitStack() as ctx:
        keep = ctx.enter_context(tc.tile_pool(name="keep", bufs=1))
        stage = ctx.enter_context(tc.tile_pool(name="stage", bufs=3))
        outs = ctx.enter_context(tc.tile_pool(name="outs", bufs=4))
        psum = ctx.enter_context(tc.psum_pool(name="psum", bufs=8))
        ctx.enter_context(tc.manual_schedule())

        shapes_rows = shapes_bytes.rearrange("(p i) k -> p i k", i=TILES)
        flex_rows = flex.rearrange("(p i) l -> p i l", i=TILES)
        u_rows = out_0.rearrange("(p i) t -> p i t", i=TILES)
        r_rows = out_1.rearrange("(p i) t -> p i t", i=TILES)

        loads_raw = keep.tile([P, 4, T], U8, name="loads_raw", align_bytes=64)
        ls_all = keep.tile([P, 32], F32, name="ls_all")
        ls = keep.tile([P, 8], F32, name="ls")
        ss = keep.tile([P, TILES, 8], F32, name="ss")
        gap_raw = keep.tile([P, TILES], BF16, name="gap_raw")
        stiff_raw = keep.tile([P, TILES], BF16, name="stiff_raw")
        neg_gap = keep.tile([P, TILES], F32, name="neg_gap")
        stiff_f = keep.tile([P, TILES], F32, name="stiff_f")
        ident = keep.tile([P, P], F32, name="ident")
        mov_codes = keep.tile([P, 3, T], U32, name="mov_codes", align_bytes=64)
        mov_scales = keep.tile([P, 3, T], U8, name="mov_scales", align_bytes=64)

        shapes_raw, flex_raw, coords_raw = {}, {}, {}

        def load_shapes(n):
            lo, hi = ROW_CHUNKS[n]
            s_tile = keep.tile([P, hi - lo, K], U8, name="shapes_raw%d" % n, align_bytes=64)
            nc.sync.dma_start(out=s_tile[:], in_=shapes_rows[:, lo:hi, :])
            for i in range(lo, hi):
                shapes_raw[i] = s_tile[:, i - lo, :]

        def load_flex(n):
            lo, hi = ROW_CHUNKS[n]
            f_tile = keep.tile([P, hi - lo, L], BF16, name="flex_raw%d" % n, align_bytes=64)
            nc.sync.dma_start(out=f_tile[:], in_=flex_rows[:, lo:hi, :])
            for i in range(lo, hi):
                flex_raw[i] = f_tile[:, i - lo, :]

        def load_coords(c):
            c_tile = keep.tile([P, 2, K], BF16, name="coords_raw%d" % c, align_bytes=64)
            nc.sync.dma_start(out=c_tile[:], in_=coords[256 * c : 256 * (c + 1), :].rearrange("(p j) k -> p j k", j=2))
            coords_raw[c] = c_tile


        loads_wide, loads_grouped, coords_grouped = {}, {}, {}
        sums = {}
        wide, turned, grouped, codes, scales, u_out, r_out = {}, {}, {}, {}, {}, {}, {}

        def widen_loads(h, blocks, on_scalar):
            if h not in loads_wide:
                loads_wide[h] = keep.tile([P, 4, HALF], BF16, name="loads_wide%d" % h, align_bytes=64)
            for b in blocks:
                for t in range(4):
                    j = 4 * h + b
                    src = loads_raw[:, t, B * j : B * (j + 1)].bitcast(FP8)
                    dst = loads_wide[h][:, t, B * b : B * (b + 1)]
                    if on_scalar:
                        nc.scalar.activation(out=dst, in_=src, func=ACT.Copy, scale=ls[:, j : j + 1])
                    else:
                        nc.vector.tensor_scalar(out=dst, in0=src, scalar1=ls[:, j : j + 1], scalar2=None, op0=ALU.mult)

        def interleave_loads(h):
            loads_grouped[h] = keep.tile([P, HALF, 4], BF16, name="loads_grouped%d" % h, align_bytes=64)
            nc.vector.tensor_copy(
                out=loads_grouped[h][:].rearrange("p (c i) t -> p c t i", i=4),
                in_=loads_wide[h][:].rearrange("p t (c i) -> p c t i", i=4),
            )

        def quantize_moving(g, h, src):
            cols = slice(HALF * h, HALF * (h + 1))
            nc.vector.quantize_mx(out=mov_codes[:, g, cols].bitcast(FP8X4), scales=mov_scales[:, g, cols], in_=src)

        def quantize_loads(h):
            quantize_moving(2, h, loads_grouped[h][:].rearrange("p c t -> p (c t)"))

        def turn_coords(c):
            for g in range(2):
                bank = psum.tile([P, 2, 2, P], F32, name="bank")
                for j in range(2):
                    words = coords_raw[c][:, j, :].bitcast(F32)
                    for u in range(2):
                        nc.tensor.transpose(bank[:, j, u, :], words[:, 256 * g + u : 256 * (g + 1) : 2], ident[:])
                turned["coords", c, g] = bank

        def empty_coords(c):
            h = c // 2
            for g in range(2):
                if (h, g) not in coords_grouped:
                    coords_grouped[h, g] = keep.tile([P, 2, 1024], BF16, name="coords_grouped%d%d" % (h, g), align_bytes=64)
                dst = coords_grouped[h, g][:, c % 2, :].bitcast(F32).rearrange("q (p j u) -> q p j u", j=2, u=2)
                nc.scalar.copy(out=dst, in_=turned["coords", c, g][:].rearrange("q j u p -> q p j u"))

        def quantize_coords(h, g):
            quantize_moving(g, h, coords_grouped[h, g][:].rearrange("q c n -> q (c n)"))

        def widen_shapes(i):
            wide[i] = stage.tile([P, 2, 2, P, 2], BF16, name="wide", bufs=6, align_bytes=64)
            for b in range(8):
                g, q = divmod(b, 4)
                src = shapes_raw[i][:, B * b : B * (b + 1)].bitcast(FP8).rearrange("p (w u e) -> p w u e", u=2, e=2)
                dst = wide[i][:, g, :, 32 * q : 32 * (q + 1), :].rearrange("p u w e -> p w u e")
                nc.vector.tensor_scalar(out=dst, in0=src, scalar1=ss[:, i, b : b + 1], scalar2=None, op0=ALU.mult)

        def widen_plain(i):
            wide[i] = keep.tile([P, K], BF16, name="plain%d" % i, align_bytes=64)
            for b in range(8):
                cols = slice(B * b, B * (b + 1))
                nc.scalar.activation(
                    out=wide[i][:, cols], in_=shapes_raw[i][:, cols].bitcast(FP8), func=ACT.Copy, scale=ss[:, i, b : b + 1]
                )

        def turn_plain(i):
            bank = psum.tile([P, 2, 2, P], F32, name="bank")
            words = wide[i][:].bitcast(F32)
            for g in range(2):
                for u in range(2):
                    nc.tensor.transpose(bank[:, g, u, :], words[:, 256 * g + u : 256 * (g + 1) : 2], ident[:])
            turned[i // 2, i % 2] = bank

        def turn_shapes(i):
            bank = psum.tile([P, 2, 2, P], F32, name="bank")
            for g in range(2):
                for u in range(2):
                    words = wide[i][:, g, u, :, :].rearrange("p w e -> p (w e)").bitcast(F32)
                    nc.tensor.transpose(bank[:, g, u, :], words, ident[:])
            turned[i // 2, i % 2] = bank

        def turn_flex(j):
            bank = psum.tile([P, 2, 2, P], F32, name="bank")
            for a in range(2):
                words = flex_raw[2 * j + a].bitcast(F32)
                for u in range(2):
                    nc.tensor.transpose(bank[:, a, u, :], words[:, u:256:2], ident[:])
            turned[j, 2] = bank

        def turn_pair(j):
            turn_shapes(2 * j)
            turn_shapes(2 * j + 1)
            turn_flex(j)

        def empty(j, n):
            if j not in grouped:
                grouped[j] = stage.tile([P, 3, 1024], BF16, name="grouped", align_bytes=64)
            dst = grouped[j][:, n, :].bitcast(F32).rearrange("q (x r u) -> q x r u", x=2, u=2)
            nc.scalar.copy(out=dst, in_=turned[j, n][:].rearrange("q x u r -> q x r u"))

        def empty_pair(j):
            for n in range(3):
                empty(j, n)

        def open_codes(j):
            if j not in codes:
                codes[j] = stage.tile([P, 6 * P], U32, name="codes", align_bytes=64)
                scales[j] = stage.tile([P, 6 * P], U8, name="scales", align_bytes=64)

        def quantize_shapes(j):
            open_codes(j)
            nc.vector.quantize_mx(
                out=codes[j][:, : 4 * P].bitcast(FP8X4),
                scales=scales[j][:, : 4 * P],
                in_=grouped[j][:, 0:2, :].rearrange("q n c -> q (n c)"),
            )

        def quantize_tile(j, a):
            open_codes(j)
            cols = slice(2 * P * a, 2 * P * (a + 1))
            nc.vector.quantize_mx(out=codes[j][:, cols].bitcast(FP8X4), scales=scales[j][:, cols], in_=grouped[j][:, a, :])

        def quantize_flex(j):
            open_codes(j)
            nc.vector.quantize_mx(
                out=codes[j][:, 4 * P :].bitcast(FP8X4), scales=scales[j][:, 4 * P :], in_=grouped[j][:, 2, :]
            )

        def multiply(j, a, h):
            if j not in u_out:
                u_out[j] = outs.tile([P, 2, T], F32, name="u_out")
                r_out[j] = outs.tile([P, 2, T], F32, name="r_out")
            cols = slice(HALF * h, HALF * (h + 1))
            bank = psum.tile([P, HALF], F32, name="bank")
            for g in range(3):
                slot = 2 * a + g if g < 2 else 4 + a
                rows = slice(P * slot, P * (slot + 1))
                nc.tensor.matmul_mx(
                    out=bank[:],
                    lhsT=codes[j][:, rows].bitcast(FP8X4),
                    lhsT_scale=scales[j][:, rows],
                    rhs=mov_codes[:, g, cols].bitcast(FP8X4),
                    rhs_scale=mov_scales[:, g, cols],
                    start=(g == 0),
                    stop=(g == 2),
                )
            sums[j, a, h] = bank

        def drain(j, a, h):
            cols = slice(HALF * h, HALF * (h + 1))
            bank = sums[j, a, h]
            nc.scalar.copy(out=u_out[j][:, a, cols], in_=bank[:])

        def close_gap_scalar(j, a, h):
            i = 2 * j + a
            cols = slice(HALF * h, HALF * (h + 1))
            nc.scalar.activation(
                out=r_out[j][:, a, cols], in_=sums[j, a, h][:], func=ACT.Relu, bias=neg_gap[:, i : i + 1]
            )

        def close_gap(j, a, lo, hi):
            i = 2 * j + a
            cols = slice(HALF * lo, HALF * hi)
            nc.vector.tensor_scalar(
                out=r_out[j][:, a, cols], in0=u_out[j][:, a, cols], scalar1=neg_gap[:, i : i + 1], scalar2=0.0,
                op0=ALU.add, op1=ALU.max,
            )

        def react(j, a, lo, hi):
            i = 2 * j + a
            cols = slice(HALF * lo, HALF * hi)
            nc.vector.tensor_scalar(
                out=r_out[j][:, a, cols], in0=r_out[j][:, a, cols], scalar1=stiff_f[:, i : i + 1], scalar2=None,
                op0=ALU.mult,
            )

        def store_u(j, a, lo, hi):
            cols = slice(HALF * lo, HALF * hi)
            nc.sync.dma_start(out=u_rows[:, 2 * j + a, cols], in_=u_out[j][:, a, cols])

        def store_r(j, a, lo, hi):
            cols = slice(HALF * lo, HALF * hi)
            nc.sync.dma_start(out=r_rows[:, 2 * j + a, cols], in_=r_out[j][:, a, cols])

        def store_pair(rows, tiles, j):
            nc.sync.dma_start(out=rows[:, 2 * j : 2 * j + 2, :], in_=tiles[j][:])

        def load_loads():
            nc.sync.dma_start(out=loads_raw[:], in_=loads_bytes.rearrange("(p t) n -> p t n", t=4))

        def load_scales():
            nc.scalar.dma_start(out=ss[:], in_=shapes_scale.rearrange("(p i) b -> p i b", i=TILES))
            nc.scalar.dma_start(out=ls_all[:], in_=loads_scale.rearrange("a b -> (a b)").partition_broadcast(P))

        def prepare_tensor():
            make_identity(nc, ident[:])

        def spread_loads_scale():
            for q in range(4):
                rows = slice(32 * q, 32 * (q + 1))
                nc.vector.tensor_copy(out=ls[rows, :], in_=ls_all[rows, 8 * q : 8 * (q + 1)])

        def load_stops():
            nc.sync.dma_start(out=gap_raw[:], in_=gap.rearrange("(p i) o -> p (i o)", i=TILES))
            nc.sync.dma_start(out=stiff_raw[:], in_=stiffness.rearrange("(p i) o -> p (i o)", i=TILES))

        def widen_stops():
            nc.vector.tensor_scalar(out=neg_gap[:], in0=gap_raw[:], scalar1=-1.0, scalar2=None, op0=ALU.mult)
            nc.vector.tensor_copy(out=stiff_f[:], in_=stiff_raw[:])

        load_scales()
        prepare_tensor()
        load_shapes(0)
        load_loads()
        load_coords(0)
        load_coords(1)
        load_flex(0)
        load_coords(2)
        load_shapes(1)
        load_flex(1)
        load_coords(3)
        load_stops()
        load_shapes(2)
        load_flex(2)
        load_shapes(3)
        load_flex(3)
        load_shapes(4)
        load_flex(4)
        widen_shapes(0)
        widen_plain(1)
        spread_loads_scale()
        turn_shapes(0)
        turn_plain(1)
        turn_coords(0)
        turn_coords(1)
        turn_flex(0)
        empty(0, 0)
        widen_loads(1, [0], True)
        empty(0, 1)
        widen_loads(0, range(4), False)
        quantize_shapes(0)
        interleave_loads(0)
        empty_coords(0)
        empty_coords(1)
        turn_coords(2)
        widen_loads(1, [1], True)
        empty(0, 2)
        widen_loads(1, [2, 3], True)
        quantize_coords(0, 0)
        quantize_coords(0, 1)
        quantize_loads(0)
        quantize_flex(0)
        multiply(0, 0, 0)
        turn_coords(3)
        multiply(0, 1, 0)
        empty_coords(2)
        empty_coords(3)
        widen_shapes(2)
        interleave_loads(1)
        widen_shapes(3)
        drain(0, 0, 0)
        store_u(0, 0, 0, 1)
        drain(0, 1, 0)
        store_u(0, 1, 0, 1)
        turn_shapes(2)
        turn_shapes(3)
        turn_flex(1)
        empty(1, 0)
        empty(1, 1)
        empty(1, 2)
        quantize_coords(1, 0)
        quantize_coords(1, 1)
        quantize_loads(1)
        widen_shapes(4)
        widen_shapes(5)
        widen_stops()
        quantize_shapes(1)
        multiply(0, 0, 1)
        multiply(0, 1, 1)
        drain(0, 0, 1)
        store_u(0, 0, 1, 2)
        drain(0, 1, 1)
        store_u(0, 1, 1, 2)
        close_gap_scalar(0, 1, 1)
        close_gap(0, 0, 0, 2)
        quantize_flex(1)
        react(0, 0, 0, 2)
        close_gap(0, 1, 0, 1)
        store_r(0, 0, 0, 2)
        turn_shapes(4)
        turn_shapes(5)
        turn_flex(2)
        empty(2, 0)
        empty(2, 1)
        empty(2, 2)
        multiply(1, 0, 0)
        drain(1, 0, 0)
        multiply(1, 0, 1)
        drain(1, 0, 1)
        multiply(1, 1, 0)
        drain(1, 1, 0)
        multiply(1, 1, 1)
        drain(1, 1, 1)
        close_gap_scalar(1, 1, 1)
        widen_shapes(6)
        react(0, 1, 0, 2)
        store_r(0, 1, 0, 2)
        widen_shapes(7)
        quantize_shapes(2)
        close_gap(1, 0, 0, 2)
        quantize_flex(2)
        store_u(1, 0, 0, 2)
        store_u(1, 1, 0, 2)
        react(1, 0, 0, 2)
        store_r(1, 0, 0, 2)
        close_gap(1, 1, 0, 1)
        turn_shapes(6)
        turn_shapes(7)
        turn_flex(3)
        empty(3, 0)
        empty(3, 1)
        empty(3, 2)
        multiply(2, 0, 0)
        drain(2, 0, 0)
        multiply(2, 0, 1)
        drain(2, 0, 1)
        multiply(2, 1, 0)
        drain(2, 1, 0)
        multiply(2, 1, 1)
        drain(2, 1, 1)
        close_gap_scalar(2, 1, 1)
        widen_shapes(8)
        react(1, 1, 0, 2)
        store_r(1, 1, 0, 2)
        widen_shapes(9)
        quantize_shapes(3)
        close_gap(2, 0, 0, 2)
        quantize_flex(3)
        store_u(2, 0, 0, 2)
        store_u(2, 1, 0, 2)
        react(2, 0, 0, 2)
        store_r(2, 0, 0, 2)
        close_gap(2, 1, 0, 1)
        turn_shapes(8)
        turn_shapes(9)
        turn_flex(4)
        empty(4, 0)
        empty(4, 1)
        empty(4, 2)
        multiply(3, 0, 0)
        drain(3, 0, 0)
        multiply(3, 0, 1)
        drain(3, 0, 1)
        multiply(3, 1, 0)
        drain(3, 1, 0)
        multiply(3, 1, 1)
        drain(3, 1, 1)
        close_gap_scalar(3, 1, 1)
        widen_shapes(10)
        react(2, 1, 0, 2)
        store_r(2, 1, 0, 2)
        widen_shapes(11)
        quantize_shapes(4)
        close_gap(3, 0, 0, 2)
        quantize_flex(4)
        store_u(3, 0, 0, 2)
        store_u(3, 1, 0, 2)
        react(3, 0, 0, 2)
        store_r(3, 0, 0, 2)
        close_gap(3, 1, 0, 1)
        turn_shapes(10)
        turn_shapes(11)
        turn_flex(5)
        empty(5, 0)
        empty(5, 1)
        empty(5, 2)
        multiply(4, 0, 0)
        drain(4, 0, 0)
        multiply(4, 0, 1)
        drain(4, 0, 1)
        multiply(4, 1, 0)
        drain(4, 1, 0)
        multiply(4, 1, 1)
        drain(4, 1, 1)
        close_gap_scalar(4, 1, 1)
        widen_shapes(12)
        react(3, 1, 0, 2)
        store_r(3, 1, 0, 2)
        widen_shapes(13)
        quantize_shapes(5)
        close_gap(4, 0, 0, 2)
        quantize_flex(5)
        store_u(4, 0, 0, 2)
        store_u(4, 1, 0, 2)
        react(4, 0, 0, 2)
        store_r(4, 0, 0, 2)
        close_gap(4, 1, 0, 1)
        turn_shapes(12)
        turn_shapes(13)
        turn_flex(6)
        empty(6, 0)
        empty(6, 1)
        empty(6, 2)
        multiply(5, 0, 0)
        drain(5, 0, 0)
        multiply(5, 0, 1)
        drain(5, 0, 1)
        multiply(5, 1, 0)
        drain(5, 1, 0)
        multiply(5, 1, 1)
        drain(5, 1, 1)
        widen_shapes(14)
        react(4, 1, 0, 2)
        store_r(4, 1, 0, 2)
        widen_shapes(15)
        quantize_shapes(6)
        close_gap(5, 0, 0, 2)
        quantize_flex(6)
        store_u(5, 0, 0, 2)
        store_u(5, 1, 0, 2)
        react(5, 0, 0, 2)
        store_r(5, 0, 0, 2)
        close_gap(5, 1, 0, 2)
        turn_shapes(14)
        turn_shapes(15)
        turn_flex(7)
        empty(7, 0)
        empty(7, 1)
        empty(7, 2)
        multiply(6, 0, 0)
        drain(6, 0, 0)
        multiply(6, 0, 1)
        drain(6, 0, 1)
        multiply(6, 1, 0)
        drain(6, 1, 0)
        multiply(6, 1, 1)
        drain(6, 1, 1)
        react(5, 1, 0, 2)
        store_r(5, 1, 0, 2)
        quantize_shapes(7)
        close_gap(6, 0, 0, 2)
        quantize_flex(7)
        store_u(6, 0, 0, 2)
        store_u(6, 1, 0, 2)
        react(6, 0, 0, 2)
        store_r(6, 0, 0, 2)
        close_gap(6, 1, 0, 2)
        multiply(7, 0, 0)
        drain(7, 0, 0)
        multiply(7, 0, 1)
        drain(7, 0, 1)
        multiply(7, 1, 0)
        drain(7, 1, 0)
        multiply(7, 1, 1)
        drain(7, 1, 1)
        react(6, 1, 0, 2)
        store_r(6, 1, 0, 2)
        close_gap(7, 0, 0, 2)
        store_u(7, 0, 0, 2)
        store_u(7, 1, 0, 2)
        react(7, 0, 0, 2)
        store_r(7, 0, 0, 2)
        close_gap(7, 1, 0, 1)
        close_gap(7, 1, 1, 2)
        react(7, 1, 0, 1)
        react(7, 1, 1, 2)
        store_r(7, 1, 0, 2)
